import numpy as np
import ml_dtypes


def mxq(x, axis, fmt="e4m3"):
    dtype, down = {"e4m3": (ml_dtypes.float8_e4m3fn, 7), "e5m2": (ml_dtypes.float8_e5m2, 14)}[fmt]
    v = np.moveaxis(np.asarray(x, np.float32).astype(ml_dtypes.bfloat16).astype(np.float64), axis, -1)
    blocks = v.reshape(v.shape[:-1] + (-1, 32))
    amax = np.abs(blocks).max(-1, keepdims=True)
    byte = np.maximum(np.where(amax > 0, np.frexp(amax)[1] - 1 + 127, 0) - down, 1)
    scale = np.exp2(byte - 127.0)
    codes = (blocks / scale).astype(np.float32).astype(dtype).astype(np.float64)
    return np.moveaxis((codes * scale).reshape(v.shape), -1, axis)


WIDE = False


def mx_kscale(k):
    if not WIDE:
        return np.ones(k)
    levels = np.array([10, -10, 5, -5, 0])
    if k % 512:
        return np.exp2(np.random.permutation(np.resize(levels, k // 32))).repeat(32)
    a = np.empty((k // 512, 16))
    for p in range(k // 512):
        a[p, :8] = np.random.permutation(np.resize(levels, 8))
        for g in range(8):
            far = levels[np.abs(levels - a[p, g]) >= 10]
            a[p, g + 8] = far[np.random.randint(len(far))]
    return np.exp2(a.ravel()).repeat(32)


def f64(x):
    return np.asarray(x).astype(np.float64)


def striped(idx):
    return np.tile(np.asarray(idx).reshape(-1, 16).T, (8, 1)).astype(np.uint16)


def unstriped(offs):
    return offs[:16].T.reshape(-1).astype(np.int64)


def striped8(idx):
    return np.asarray(idx).reshape(8, -1, 16).transpose(0, 2, 1).reshape(128, -1).astype(np.uint16)


def unstriped8(offs):
    return offs.reshape(8, 16, -1).transpose(0, 2, 1).reshape(8, -1).astype(np.int64)


def pick8(x, idx, run):
    r = np.arange(len(x))
    return x[r[:, None], idx[r % (8 * run) // run]]


E2M1 = np.array([0.0, 0.5, 1.0, 1.5, 2.0, 3.0, 4.0, 6.0, -0.0, -0.5, -1.0, -1.5, -2.0, -3.0, -4.0, -6.0])


def pack_weight(w, fmt):
    k, n = w.shape
    w = f64(np.asarray(w, np.float32).astype(ml_dtypes.bfloat16)).reshape(k // 32, 32, n)
    amax = np.abs(w).max(1)
    if fmt == "e4m3":
        byte = np.frexp(amax)[1] - 1 + 127 - 7
    else:
        mant, ex = np.frexp(amax / 6.0)
        byte = np.where(mant > 0.5, ex, ex - 1) + 127
    byte = np.clip(np.where(amax > 0, byte, 1), 1, 254)
    scaled = (w * np.exp2(127.0 - byte)[:, None, :]).reshape(k, n).astype(np.float32)
    by_word = np.ascontiguousarray(scaled.reshape(k // 512, 128, 4, n).transpose(0, 1, 3, 2))
    if fmt == "e4m3":
        words = by_word.astype(ml_dtypes.float8_e4m3fn).view(np.uint8)
    else:
        c = by_word.astype(ml_dtypes.float4_e2m1fn).view(np.uint8) & 0xF
        words = (c[..., 0::2] | (c[..., 1::2] << 4)).reshape(k // 512, 128, 2 * n)
    return np.ascontiguousarray(words), np.ascontiguousarray(byte.astype(np.uint8).reshape(k // 512, 16, n))


def unpack_weight(words, scales, fmt):
    g, _, n = scales.shape
    words = np.ascontiguousarray(words).reshape(g, 128, n, -1)
    if fmt == "e4m3":
        vals = words.view(ml_dtypes.float8_e4m3fn).astype(np.float64)
    else:
        nib = np.empty((g, 128, n, 4), np.uint8)
        nib[..., 0::2] = words & 0xF
        nib[..., 1::2] = words >> 4
        vals = E2M1[nib]
    vals = vals * np.repeat(np.exp2(scales.astype(np.float64) - 127.0), 8, axis=1)[..., None]
    return vals.transpose(0, 1, 3, 2).reshape(g * 512, n)


K, J, R, T, Z, M, C, O, S, N = 512, 256, 512, 1024, 512, 1024, 512, 256, 128, 256


def setup_inputs():
    n = np.random.standard_normal
    idx = np.random.permutation(T)[:J]
    idx2 = np.random.permutation(M)[:J]
    idx3 = np.stack([np.random.permutation(C)[:J] for _ in range(8)])
    idx4 = np.stack([np.random.permutation(J)[:S] for _ in range(8)])
    idx5 = np.stack([np.random.permutation(C)[:S] for _ in range(8)])
    idx6 = np.stack([np.random.permutation(C)[:O] for _ in range(8)])
    fk = mx_kscale(K)
    fr = mx_kscale(R)
    fz = mx_kscale(Z)
    xtp = pack_weight(n((K, T)) * fk[:, None], "e2m1")
    wp = pack_weight(n((K, R)) * 1 / np.sqrt(K) / fk[:, None] * fr, "e4m3")
    xop = pack_weight(n((Z, M)) / fz[:, None], "e4m3")
    w2p = pack_weight(n((Z, R)) * 1 / np.sqrt(Z) * fz[:, None] * fr, "e2m1")
    wbp = pack_weight(n((R, N)) * 1 / np.sqrt(R) / fr[:, None], "e2m1")
    return {
        "xt_words": xtp[0],
        "xt_scales": xtp[1],
        "w_words": wp[0],
        "w_scales": wp[1],
        "xo_words": xop[0],
        "xo_scales": xop[1],
        "w2_words": w2p[0],
        "w2_scales": w2p[1],
        "sa": (np.random.uniform(0.5, 1.6, (R, 1))).astype(np.float32),
        "sb": (np.random.uniform(0.5, 1.6, (R, 1))).astype(np.float32),
        "wb_words": wbp[0],
        "wb_scales": wbp[1],
        "offs": striped(idx),
        "offs2": striped(idx2),
        "offs3": striped8(idx3),
        "offs4": striped8(idx4),
        "offs5": striped8(idx5),
        "offs6": striped8(idx6),
    }


def reference(xt_words, xt_scales, w_words, w_scales, xo_words, xo_scales, w2_words, w2_scales, sa, sb, wb_words, wb_scales, offs, offs2, offs3, offs4, offs5, offs6):
    idx = unstriped(offs)
    idx2 = unstriped(offs2)
    idx3 = unstriped8(offs3)
    idx4 = unstriped8(offs4)
    idx5 = unstriped8(offs5)
    idx6 = unstriped8(offs6)
    xtu = unpack_weight(xt_words, xt_scales, "e2m1")
    wu = unpack_weight(w_words, w_scales, "e4m3")
    xou = unpack_weight(xo_words, xo_scales, "e4m3")
    w2u = unpack_weight(w2_words, w2_scales, "e2m1")
    wbu = unpack_weight(wb_words, wb_scales, "e2m1")
    xtidxg = xtu[:, idx]
    xoidx2g = xou[:, idx2]
    a = wu.T @ xtidxg + w2u.T @ xoidx2g
    pw = np.zeros((R, C))
    pw[np.arange(R)[:, None], idx3[np.arange(R) % 512 // 64]] = a
    h1 = pick8(a, idx4, 64) * f64(sa)
    pv = np.zeros((R, C))
    pv[np.arange(R)[:, None], idx5[np.arange(R) % 512 // 64]] = h1
    pb = np.max(pv, axis=1, keepdims=True)
    pg = np.maximum(pw, pv - pb)
    hid = pick8(pg, idx6, 64) * f64(sb)
    hidq = mxq(hid, 0, "e4m3")
    y = wbu.T @ hidq
    return y

@@ -1,0 +1,212 @@
+from contextlib import ExitStack
+
+import concourse.mybir as mybir
+
+K, J, R, T, Z, M, C, O, S, N = 512, 256, 512, 1024, 512, 1024, 512, 256, 128, 256
+FLOPS = 2 * (K * R * J + Z * R * J + R * N * O)
+
+F32 = mybir.dt.float32
+BF16 = mybir.dt.bfloat16
+I32 = mybir.dt.int32
+U32 = mybir.dt.uint32
+U16 = mybir.dt.uint16
+U8 = mybir.dt.uint8
+FP8X4 = mybir.dt.float8_e4m3fn_x4
+FP4X4 = mybir.dt.float4_e2m1fn_x4
+ALU = mybir.AluOpType
+COPY = mybir.ActivationFunctionType.Copy
+AX = mybir.AxisListType.X
+
+P = 128
+PACK = 4
+HALF = O // 2
+
+
+def tile_picked_tokens_plain_bank_belowbest_one_plain_kernel(tc, xt_words, xt_scales, w_words, w_scales, xo_words, xo_scales, w2_words, w2_scales, sa, sb, wb_words, wb_scales, offs, offs2, offs3, offs4, offs5, offs6, out):
+    nc = tc.nc
+    with ExitStack() as ctx:
+        keep = ctx.enter_context(tc.tile_pool(name="keep", bufs=1))
+        psum = ctx.enter_context(tc.psum_pool(name="psum", bufs=1))
+
+        def held(shape, dtype, name, tag=None):
+            return keep.tile(shape, dtype, name=name, tag=tag or name, align_bytes=64)
+
+        def load_list(src, name):
+            lst = keep.tile([P, src.shape[1]], U16, name=name)
+            nc.sync.dma_start(lst[:], src)
+            return lst
+
+        def zeroed_plane(width, name):
+            plane = held([P, width], U8, name)
+            nc.vector.memset(plane[:].bitcast(U32), 0)
+            return plane
+
+        def load_plane(queue, plane, scales):
+            for q in range(4):
+                queue.dma_start(plane[32 * q : 32 * q + 4, :].bitcast(I32), scales[0, 4 * q : 4 * q + 4, :].bitcast(I32))
+
+        xt_plane = zeroed_plane(T, "xt_plane")
+        ws_plane = zeroed_plane(2 * R, "ws_plane")
+        xo_plane = zeroed_plane(M, "xo_plane")
+        wb_plane = zeroed_plane(N, "wb_plane")
+        xt_stage = held([4, 4, T], U8, "xt_stage")
+        ws_stage = held([4, 4, 2, R], U8, "ws_stage")
+
+        xt_win = held([P, T], U16, "xt_win")
+        xo_win = held([P, M], U32, "xo_win")
+        w_raw = held([P, R], U32, "w_raw")
+        w2_raw = held([P, R], U16, "w2_raw")
+        wb_codes = held([P, N], U16, "wb_codes")
+        sa_t = held([P, PACK], F32, "sa_t")
+        sb_t = held([P, PACK], F32, "sb_t")
+
+        def by_quadrant(scales):
+            return scales[0].bitcast(I32).rearrange("(q i) c -> i q c", i=4)
+
+        l1 = load_list(offs, "l1")
+        nc.sync.dma_start(xt_stage[:].bitcast(I32), by_quadrant(xt_scales))
+        nc.sync.dma_start(xt_win[:].bitcast(I32), xt_words[0].bitcast(I32))
+        l2 = load_list(offs2, "l2")
+        nc.sync.dma_start(ws_stage[:, :, 0, :].bitcast(I32), by_quadrant(w_scales))
+        nc.sync.dma_start(ws_stage[:, :, 1, :].bitcast(I32), by_quadrant(w2_scales))
+        nc.sync.dma_start(xo_win[:].bitcast(I32), xo_words[0].rearrange("p n t -> p (n t)").bitcast(I32))
+        nc.sync.dma_start(w_raw[:].bitcast(I32), w_words[0].rearrange("p n t -> p (n t)").bitcast(I32))
+        nc.sync.dma_start(w2_raw[:].bitcast(I32), w2_words[0].bitcast(I32))
+        load_plane(nc.sync, xo_plane, xo_scales)
+        l3 = load_list(offs3, "l3")
+        l4 = load_list(offs4, "l4")
+        nc.sync.dma_start(sa_t[:], sa.rearrange("(p t) one -> p (t one)", t=PACK))
+        l5 = load_list(offs5, "l5")
+        l6 = load_list(offs6, "l6")
+        nc.sync.dma_start(sb_t[:], sb.rearrange("(p t) one -> p (t one)", t=PACK))
+        nc.sync.dma_start(wb_codes[:].bitcast(I32), wb_words[0].bitcast(I32))
+        load_plane(nc.sync, wb_plane, wb_scales)
+
+        xt_gs = held([P, J], U8, "xt_gs")
+        xt_g = held([P, J], U16, "xt_g")
+        xo_g = held([P, J], U32, "xo_g")
+        xo_gs = held([P, J], U8, "xo_gs")
+        for q in range(4):
+            nc.vector.tensor_copy(xt_plane[32 * q : 32 * q + 4, :].bitcast(I32), xt_stage[:, q, :].bitcast(I32))
+        nc.vector.tensor_copy(xt_g[:], xt_win[:].indirect(l1[:]))
+        nc.vector.tensor_copy(xt_gs[:], xt_plane[:].indirect(l1[:]))
+        for q in range(4):
+            nc.vector.tensor_copy(ws_plane[32 * q : 32 * q + 4, :].bitcast(I32), ws_stage[:, q].rearrange("i w c -> i (w c)").bitcast(I32))
+        nc.vector.tensor_copy(xo_g[:], xo_win[:].indirect(l2[:]))
+
+        ws_first = held([P, 2, P], U8, "ws_first")
+        ws_by_t = ws_plane[:].rearrange("p (w m t) -> p w t m", w=2, t=PACK)
+        nc.vector.tensor_copy(ws_first[:], ws_by_t[:, :, 0, :])
+        nc.vector.tensor_copy(xo_gs[:], xo_plane[:].indirect(l2[:]))
+
+        dealt = []
+        for raw, dtype, name in ((w_raw, U32, "w_d"), (w2_raw, U16, "w2_d")):
+            first = held([P, P], dtype, name + "_first")
+            rest = held([P, PACK - 1, P], dtype, name + "_rest")
+            by_t = raw[:].rearrange("p (m t) -> p m t", t=PACK)
+            nc.scalar.copy(first[:], by_t[:, :, 0])
+            dealt.append((first, rest, by_t))
+
+        def cols(i, t):
+            if i >= 2:
+                return ws_first[:, i - 2, :] if t == 0 else ws_rest[:, t - 1, i - 2, :]
+            return dealt[i][0][:] if t == 0 else dealt[i][1][:, t - 1, :]
+
+        a_tiles = []
+
+        def hidden(t):
+            acc = psum.tile([P, J], F32, name="acc%d" % t)
+            nc.tensor.matmul_mx(acc[:], lhsT=cols(0, t).bitcast(FP8X4), lhsT_scale=cols(2, t),
+                                rhs=xt_g[:].bitcast(FP4X4), rhs_scale=xt_gs[:], start=True, stop=False)
+            nc.tensor.matmul_mx(acc[:], lhsT=cols(1, t).bitcast(FP4X4), lhsT_scale=cols(3, t),
+                                rhs=xo_g[:].bitcast(FP8X4), rhs_scale=xo_gs[:], start=False, stop=True)
+            a = held([P, J], F32, "a%d" % t)
+            nc.vector.tensor_copy(a[:], acc[:])
+            a_tiles.append(a)
+
+        hidden(0)
+        for first, rest, by_t in dealt:
+            nc.scalar.copy(rest[:].rearrange("p t m -> p m t"), by_t[:, :, 1:PACK])
+        ws_rest = held([P, PACK - 1, 2, P], U8, "ws_rest", "ws_first")
+        for t in range(1, PACK):
+            nc.vector.tensor_copy(ws_rest[:, t - 1], ws_by_t[:, :, t, :])
+            hidden(t)
+
+        pw_tiles, h1_tiles, pb_tiles, pg_tiles = {}, {}, {}, {}
+
+        def put_board(t):
+            pw = held([P, C], F32, "pw%d" % t, ("pw0", "w2_d_first", "w_d_rest", "h1_1")[t])
+            nc.vector.memset(pw[:], 0.0)
+            nc.scalar.activation(pw[:].indirect(l3[:]), a_tiles[t][:], COPY)
+            pw_tiles[t] = pw
+
+        def fetch_marks(t):
+            h1 = held([P, S], F32, "h1_%d" % t)
+            nc.scalar.activation(h1[:], a_tiles[t][:].indirect(l4[:]), COPY, scale=sa_t[:, t : t + 1])
+            top = held([P, 1], F32, "top%d" % t)
+            pb = held([P, 1], F32, "pb%d" % t)
+            nc.vector.tensor_reduce(top[:], h1[:], AX, ALU.max)
+            nc.vector.tensor_scalar(pb[:], top[:], 0.0, None, ALU.max)
+            h1_tiles[t], pb_tiles[t] = h1, pb
+
+        pv_tiles = {}
+
+        def put_marks(t):
+            pv = held([P, C], F32, "pv%d" % t, ("pv0", "ws_first", "w2_d_rest", "h1_0")[t])
+            nc.vector.memset(pv[:], 0.0)
+            nc.scalar.activation(pv[:].indirect(l5[:]), h1_tiles[t][:], COPY)
+            pv_tiles[t] = pv
+
+        def join(t):
+            pg = held([P, C], F32, "pg%d" % t)
+            nc.vector.scalar_tensor_tensor(pg[:], pv_tiles[t][:], pb_tiles[t][:], pw_tiles[t][:], ALU.subtract, ALU.max)
+            pg_tiles[t] = pg
+
+        put_board(0)
+        fetch_marks(0)
+        fetch_marks(1)
+        put_marks(0)
+        join(0)
+        put_board(1)
+        put_marks(1)
+        join(1)
+        fetch_marks(2)
+        put_board(2)
+        fetch_marks(3)
+        put_marks(2)
+        join(2)
+        put_marks(3)
+        put_board(3)
+        join(3)
+
+        out_v = out.rearrange("(u p) o -> p u o", p=P)
+        for h in range(2):
+            places = slice(h * HALF, (h + 1) * HALF)
+            hb = held([P, PACK, HALF], BF16, "hb%d" % h, ("h1_3", "pb3")[h])
+            lst = l6[:, h * HALF // 16 : (h + 1) * HALF // 16]
+            for t in range(PACK):
+                nc.scalar.activation(hb[:, t, :], pg_tiles[t][:].indirect(lst), COPY, scale=sb_t[:, t : t + 1])
+            woven = held([P, HALF, PACK], BF16, "woven%d" % h)
+            nc.vector.tensor_copy(woven[:].rearrange("p (c i) t -> p c t i", i=4), hb[:].rearrange("p t (c i) -> p c t i", i=4))
+            codes = held([P, HALF], U32, "codes%d" % h)
+            plane = held([P, HALF], U8, "plane%d" % h)
+            nc.vector.quantize_mx(codes[:].bitcast(FP8X4), plane[:], woven[:].rearrange("p c t -> p (c t)"))
+
+            def product(y, u):
+                nc.tensor.matmul_mx(y, lhsT=wb_codes[:, u * P : (u + 1) * P].bitcast(FP4X4), lhsT_scale=wb_plane[:, u * P : (u + 1) * P],
+                                    rhs=codes[:].bitcast(FP8X4), rhs_scale=plane[:], start=True, stop=True)
+
+            if h == 0:
+                y = psum.tile([P, 2, HALF], F32, name="y0")
+                res = held([P, 2, HALF], F32, "res0")
+                for u in range(2):
+                    product(y[:, u, :], u)
+                nc.vector.tensor_copy(res[:], y[:])
+                nc.sync.dma_start(out_v[:, :, places], res[:])
+            else:
+                for u, copy, queue in ((0, nc.vector.tensor_copy, nc.sync), (1, nc.scalar.copy, nc.scalar)):
+                    y = psum.tile([P, HALF], F32, name="y1%d" % u)
+                    res = held([P, HALF], F32, "res1%d" % u)
+                    product(y[:], u)
+                    copy(res[:], y[:])
+                    queue.dma_start(out_v[:, u, places], res[:])

@@ -49,7 +49,6 @@ def tile_picked_tokens_plain_bank_belowbest_one_plain_kernel(tc, xt_words, xt_sc
         ws_plane = zeroed_plane(2 * R, "ws_plane")
         xo_plane = zeroed_plane(M, "xo_plane")
         wb_plane = zeroed_plane(N, "wb_plane")
-        xt_stage = held([4, 4, T], U8, "xt_stage")
         ws_stage = held([4, 4, 2, R], U8, "ws_stage")
 
         xt_win = held([P, T], U16, "xt_win")
@@ -64,18 +63,18 @@ def tile_picked_tokens_plain_bank_belowbest_one_plain_kernel(tc, xt_words, xt_sc
             return scales[0].bitcast(I32).rearrange("(q i) c -> i q c", i=4)
 
         l1 = load_list(offs, "l1")
-        nc.sync.dma_start(xt_stage[:].bitcast(I32), by_quadrant(xt_scales))
-        nc.sync.dma_start(xt_win[:].bitcast(I32), xt_words[0].bitcast(I32))
-        l2 = load_list(offs2, "l2")
         nc.sync.dma_start(ws_stage[:, :, 0, :].bitcast(I32), by_quadrant(w_scales))
         nc.sync.dma_start(ws_stage[:, :, 1, :].bitcast(I32), by_quadrant(w2_scales))
-        nc.sync.dma_start(xo_win[:].bitcast(I32), xo_words[0].rearrange("p n t -> p (n t)").bitcast(I32))
+        l2 = load_list(offs2, "l2")
+        nc.sync.dma_start(xt_win[:].bitcast(I32), xt_words[0].bitcast(I32))
         nc.sync.dma_start(w_raw[:].bitcast(I32), w_words[0].rearrange("p n t -> p (n t)").bitcast(I32))
+        load_plane(nc.sync, xt_plane, xt_scales)
+        nc.sync.dma_start(xo_win[:].bitcast(I32), xo_words[0].rearrange("p n t -> p (n t)").bitcast(I32))
         nc.sync.dma_start(w2_raw[:].bitcast(I32), w2_words[0].bitcast(I32))
         load_plane(nc.sync, xo_plane, xo_scales)
-        l3 = load_list(offs3, "l3")
         l4 = load_list(offs4, "l4")
         nc.sync.dma_start(sa_t[:], sa.rearrange("(p t) one -> p (t one)", t=PACK))
+        l3 = load_list(offs3, "l3")
         l5 = load_list(offs5, "l5")
         l6 = load_list(offs6, "l6")
         nc.sync.dma_start(sb_t[:], sb.rearrange("(p t) one -> p (t one)", t=PACK))
@@ -87,16 +86,13 @@ def tile_picked_tokens_plain_bank_belowbest_one_plain_kernel(tc, xt_words, xt_sc
         xo_g = held([P, J], U32, "xo_g")
         xo_gs = held([P, J], U8, "xo_gs")
         for q in range(4):
-            nc.vector.tensor_copy(xt_plane[32 * q : 32 * q + 4, :].bitcast(I32), xt_stage[:, q, :].bitcast(I32))
-        nc.vector.tensor_copy(xt_g[:], xt_win[:].indirect(l1[:]))
-        nc.vector.tensor_copy(xt_gs[:], xt_plane[:].indirect(l1[:]))
-        for q in range(4):
             nc.vector.tensor_copy(ws_plane[32 * q : 32 * q + 4, :].bitcast(I32), ws_stage[:, q].rearrange("i w c -> i (w c)").bitcast(I32))
-        nc.vector.tensor_copy(xo_g[:], xo_win[:].indirect(l2[:]))
-
+        nc.vector.tensor_copy(xt_g[:], xt_win[:].indirect(l1[:]))
         ws_first = held([P, 2, P], U8, "ws_first")
         ws_by_t = ws_plane[:].rearrange("p (w m t) -> p w t m", w=2, t=PACK)
         nc.vector.tensor_copy(ws_first[:], ws_by_t[:, :, 0, :])
+        nc.vector.tensor_copy(xt_gs[:], xt_plane[:].indirect(l1[:]))
+        nc.vector.tensor_copy(xo_g[:], xo_win[:].indirect(l2[:]))
         nc.vector.tensor_copy(xo_gs[:], xo_plane[:].indirect(l2[:]))
 
         dealt = []
@@ -109,7 +105,9 @@ def tile_picked_tokens_plain_bank_belowbest_one_plain_kernel(tc, xt_words, xt_sc
 
         def cols(i, t):
             if i >= 2:
-                return ws_first[:, i - 2, :] if t == 0 else ws_rest[:, t - 1, i - 2, :]
+                if t == 0:
+                    return ws_first[:, i - 2, :]
+                return ws_second[:, i - 2, :] if t == 1 else ws_rest[:, t - 2, i - 2, :]
             return dealt[i][0][:] if t == 0 else dealt[i][1][:, t - 1, :]
 
         a_tiles = []
@@ -127,23 +125,30 @@ def tile_picked_tokens_plain_bank_belowbest_one_plain_kernel(tc, xt_words, xt_sc
         hidden(0)
         for first, rest, by_t in dealt:
             nc.scalar.copy(rest[:].rearrange("p t m -> p m t"), by_t[:, :, 1:PACK])
-        ws_rest = held([P, PACK - 1, 2, P], U8, "ws_rest", "ws_first")
+        ws_second = held([P, 2, P], U8, "ws_second", "ws_first")
+        ws_rest = held([P, 2, 2, P], U8, "ws_rest", "w2_d_first")
         for t in range(1, PACK):
-            nc.vector.tensor_copy(ws_rest[:, t - 1], ws_by_t[:, :, t, :])
+            nc.vector.tensor_copy(ws_second[:] if t == 1 else ws_rest[:, t - 2], ws_by_t[:, :, t, :])
             hidden(t)
+
+        pw_boards, pv_boards = [], []
+        for boards, name in ((pw_boards, "pw"), (pv_boards, "pv")):
+            for i in range(2):
+                board = held([P, C], F32, "%s%d" % (name, i))
+                nc.vector.memset(board[:].bitcast(I32), 0)
+                boards.append(board)
 
         pw_tiles, h1_tiles, pb_tiles, pg_tiles = {}, {}, {}, {}
 
         def put_board(t):
-            pw = held([P, C], F32, "pw%d" % t, ("pw0", "w2_d_first", "w_d_rest", "h1_1")[t])
-            nc.vector.memset(pw[:], 0.0)
+            pw = pw_boards[t % 2]
             nc.scalar.activation(pw[:].indirect(l3[:]), a_tiles[t][:], COPY)
             pw_tiles[t] = pw
 
         def fetch_marks(t):
             h1 = held([P, S], F32, "h1_%d" % t)
             nc.scalar.activation(h1[:], a_tiles[t][:].indirect(l4[:]), COPY, scale=sa_t[:, t : t + 1])
-            top = held([P, 1], F32, "top%d" % t)
+            top = held([P, 1], F32, "top%d" % t, "ws_first" if t == 0 else "w_d_rest")
             pb = held([P, 1], F32, "pb%d" % t)
             nc.vector.tensor_reduce(top[:], h1[:], AX, ALU.max)
             nc.vector.tensor_scalar(pb[:], top[:], 0.0, None, ALU.max)
@@ -152,8 +157,7 @@ def tile_picked_tokens_plain_bank_belowbest_one_plain_kernel(tc, xt_words, xt_sc
         pv_tiles = {}
 
         def put_marks(t):
-            pv = held([P, C], F32, "pv%d" % t, ("pv0", "ws_first", "w2_d_rest", "h1_0")[t])
-            nc.vector.memset(pv[:], 0.0)
+            pv = pv_boards[t % 2]
             nc.scalar.activation(pv[:].indirect(l5[:]), h1_tiles[t][:], COPY)
             pv_tiles[t] = pv
 
@@ -162,11 +166,11 @@ def tile_picked_tokens_plain_bank_belowbest_one_plain_kernel(tc, xt_words, xt_sc
             nc.vector.scalar_tensor_tensor(pg[:], pv_tiles[t][:], pb_tiles[t][:], pw_tiles[t][:], ALU.subtract, ALU.max)
             pg_tiles[t] = pg
 
-        put_board(0)
         fetch_marks(0)
-        fetch_marks(1)
+        put_board(0)
         put_marks(0)
         join(0)
+        fetch_marks(1)
         put_board(1)
         put_marks(1)
         join(1)

@@ -20,6 +20,7 @@ AX = mybir.AxisListType.X
 P = 128
 PACK = 4
 HALF = O // 2
+HALVES = ((slice(0, 128), slice(0, 8)), (slice(128, 256), slice(8, 16)))
 
 
 def tile_picked_tokens_plain_bank_belowbest_one_plain_kernel(tc, xt_words, xt_scales, w_words, w_scales, xo_words, xo_scales, w2_words, w2_scales, sa, sb, wb_words, wb_scales, offs, offs2, offs3, offs4, offs5, offs6, out):
@@ -41,9 +42,9 @@ def tile_picked_tokens_plain_bank_belowbest_one_plain_kernel(tc, xt_words, xt_sc
             nc.vector.memset(plane[:].bitcast(U32), 0)
             return plane
 
-        def load_plane(queue, plane, scales):
+        def load_plane(plane, scales):
             for q in range(4):
-                queue.dma_start(plane[32 * q : 32 * q + 4, :].bitcast(I32), scales[0, 4 * q : 4 * q + 4, :].bitcast(I32))
+                nc.sync.dma_start(plane[32 * q : 32 * q + 4, :].bitcast(I32), scales[0, 4 * q : 4 * q + 4, :].bitcast(I32))
 
         xt_plane = zeroed_plane(T, "xt_plane")
         ws_plane = zeroed_plane(2 * R, "ws_plane")
@@ -65,21 +66,21 @@ def tile_picked_tokens_plain_bank_belowbest_one_plain_kernel(tc, xt_words, xt_sc
         l1 = load_list(offs, "l1")
         nc.sync.dma_start(ws_stage[:, :, 0, :].bitcast(I32), by_quadrant(w_scales))
         nc.sync.dma_start(ws_stage[:, :, 1, :].bitcast(I32), by_quadrant(w2_scales))
-        l2 = load_list(offs2, "l2")
         nc.sync.dma_start(xt_win[:].bitcast(I32), xt_words[0].bitcast(I32))
+        l2 = load_list(offs2, "l2")
         nc.sync.dma_start(w_raw[:].bitcast(I32), w_words[0].rearrange("p n t -> p (n t)").bitcast(I32))
-        load_plane(nc.sync, xt_plane, xt_scales)
+        load_plane(xt_plane, xt_scales)
         nc.sync.dma_start(xo_win[:].bitcast(I32), xo_words[0].rearrange("p n t -> p (n t)").bitcast(I32))
         nc.sync.dma_start(w2_raw[:].bitcast(I32), w2_words[0].bitcast(I32))
-        load_plane(nc.sync, xo_plane, xo_scales)
+        load_plane(xo_plane, xo_scales)
+        l3 = load_list(offs3, "l3")
         l4 = load_list(offs4, "l4")
         nc.sync.dma_start(sa_t[:], sa.rearrange("(p t) one -> p (t one)", t=PACK))
-        l3 = load_list(offs3, "l3")
         l5 = load_list(offs5, "l5")
         l6 = load_list(offs6, "l6")
         nc.sync.dma_start(sb_t[:], sb.rearrange("(p t) one -> p (t one)", t=PACK))
         nc.sync.dma_start(wb_codes[:].bitcast(I32), wb_words[0].bitcast(I32))
-        load_plane(nc.sync, wb_plane, wb_scales)
+        load_plane(wb_plane, wb_scales)
 
         xt_gs = held([P, J], U8, "xt_gs")
         xt_g = held([P, J], U16, "xt_g")
@@ -92,8 +93,9 @@ def tile_picked_tokens_plain_bank_belowbest_one_plain_kernel(tc, xt_words, xt_sc
         ws_by_t = ws_plane[:].rearrange("p (w m t) -> p w t m", w=2, t=PACK)
         nc.vector.tensor_copy(ws_first[:], ws_by_t[:, :, 0, :])
         nc.vector.tensor_copy(xt_gs[:], xt_plane[:].indirect(l1[:]))
-        nc.vector.tensor_copy(xo_g[:], xo_win[:].indirect(l2[:]))
-        nc.vector.tensor_copy(xo_gs[:], xo_plane[:].indirect(l2[:]))
+        for slots, entries in HALVES:
+            nc.vector.tensor_copy(xo_g[:, slots], xo_win[:].indirect(l2[:, entries]))
+            nc.vector.tensor_copy(xo_gs[:, slots], xo_plane[:].indirect(l2[:, entries]))
 
         dealt = []
         for raw, dtype, name in ((w_raw, U32, "w_d"), (w2_raw, U16, "w2_d")):
@@ -113,13 +115,15 @@ def tile_picked_tokens_plain_bank_belowbest_one_plain_kernel(tc, xt_words, xt_sc
         a_tiles = []
 
         def hidden(t):
-            acc = psum.tile([P, J], F32, name="acc%d" % t)
-            nc.tensor.matmul_mx(acc[:], lhsT=cols(0, t).bitcast(FP8X4), lhsT_scale=cols(2, t),
-                                rhs=xt_g[:].bitcast(FP4X4), rhs_scale=xt_gs[:], start=True, stop=False)
-            nc.tensor.matmul_mx(acc[:], lhsT=cols(1, t).bitcast(FP4X4), lhsT_scale=cols(3, t),
-                                rhs=xo_g[:].bitcast(FP8X4), rhs_scale=xo_gs[:], start=False, stop=True)
             a = held([P, J], F32, "a%d" % t)
-            nc.vector.tensor_copy(a[:], acc[:])
+            for i, slots in enumerate([h[0] for h in HALVES] if t == 0 else [slice(0, J)]):
+                acc = psum.tile([P, slots.stop - slots.start], F32, name="acc%d_%d" % (t, i), tag="acc%d_%d" % (t, i))
+                nc.tensor.matmul_mx(acc[:], lhsT=cols(0, t).bitcast(FP8X4), lhsT_scale=cols(2, t),
+                                    rhs=xt_g[:, slots].bitcast(FP4X4), rhs_scale=xt_gs[:, slots], start=True, stop=False)
+                nc.tensor.matmul_mx(acc[:], lhsT=cols(1, t).bitcast(FP4X4), lhsT_scale=cols(3, t),
+                                    rhs=xo_g[:, slots].bitcast(FP8X4), rhs_scale=xo_gs[:, slots], start=False, stop=True)
+                copy = nc.vector.tensor_copy
+                copy(a[:, slots], acc[:])
             a_tiles.append(a)
 
         hidden(0)
@@ -127,22 +131,25 @@ def tile_picked_tokens_plain_bank_belowbest_one_plain_kernel(tc, xt_words, xt_sc
             nc.scalar.copy(rest[:].rearrange("p t m -> p m t"), by_t[:, :, 1:PACK])
         ws_second = held([P, 2, P], U8, "ws_second", "ws_first")
         ws_rest = held([P, 2, 2, P], U8, "ws_rest", "w2_d_first")
+        def zeroed_board(name, tag):
+            board = held([P, C], F32, name, tag)
+            nc.vector.memset(board[:].bitcast(I32), 0)
+            return board
+
+        pw_boards = [zeroed_board("pw0", "pw0")]
+        pv_boards = [zeroed_board("pv0", "pv0")]
         for t in range(1, PACK):
             nc.vector.tensor_copy(ws_second[:] if t == 1 else ws_rest[:, t - 2], ws_by_t[:, :, t, :])
             hidden(t)
-
-        pw_boards, pv_boards = [], []
-        for boards, name in ((pw_boards, "pw"), (pv_boards, "pv")):
-            for i in range(2):
-                board = held([P, C], F32, "%s%d" % (name, i))
-                nc.vector.memset(board[:].bitcast(I32), 0)
-                boards.append(board)
+            if t == 1:
+                pw_boards.append(zeroed_board("pw1", "pw1"))
+        pv_boards.append(zeroed_board("pv1", "w2_d_first"))
 
         pw_tiles, h1_tiles, pb_tiles, pg_tiles = {}, {}, {}, {}
 
-        def put_board(t):
+        def put_board(t, slots=slice(0, J), entries=slice(0, J // 16)):
             pw = pw_boards[t % 2]
-            nc.scalar.activation(pw[:].indirect(l3[:]), a_tiles[t][:], COPY)
+            nc.scalar.activation(pw[:].indirect(l3[:, entries]), a_tiles[t][:, slots], COPY)
             pw_tiles[t] = pw
 
         def fetch_marks(t):
@@ -166,8 +173,9 @@ def tile_picked_tokens_plain_bank_belowbest_one_plain_kernel(tc, xt_words, xt_sc
             nc.vector.scalar_tensor_tensor(pg[:], pv_tiles[t][:], pb_tiles[t][:], pw_tiles[t][:], ALU.subtract, ALU.max)
             pg_tiles[t] = pg
 
+        put_board(0, *HALVES[0])
         fetch_marks(0)
-        put_board(0)
+        put_board(0, *HALVES[1])
         put_marks(0)
         join(0)
         fetch_marks(1)
@@ -184,33 +192,21 @@ def tile_picked_tokens_plain_bank_belowbest_one_plain_kernel(tc, xt_words, xt_sc
         join(3)
 
         out_v = out.rearrange("(u p) o -> p u o", p=P)
-        for h in range(2):
-            places = slice(h * HALF, (h + 1) * HALF)
-            hb = held([P, PACK, HALF], BF16, "hb%d" % h, ("h1_3", "pb3")[h])
-            lst = l6[:, h * HALF // 16 : (h + 1) * HALF // 16]
-            for t in range(PACK):
-                nc.scalar.activation(hb[:, t, :], pg_tiles[t][:].indirect(lst), COPY, scale=sb_t[:, t : t + 1])
+        hb = held([P, PACK, O], BF16, "hb", "h1_3")
+        for t in range(PACK - 1):
+            nc.scalar.activation(hb[:, t, :], pg_tiles[t][:].indirect(l6[:]), COPY, scale=sb_t[:, t : t + 1])
+        for h, (places, entries) in enumerate(HALVES):
+            nc.scalar.activation(hb[:, PACK - 1, places], pg_tiles[PACK - 1][:].indirect(l6[:, entries]), COPY, scale=sb_t[:, PACK - 1 : PACK])
             woven = held([P, HALF, PACK], BF16, "woven%d" % h)
-            nc.vector.tensor_copy(woven[:].rearrange("p (c i) t -> p c t i", i=4), hb[:].rearrange("p t (c i) -> p c t i", i=4))
+            nc.vector.tensor_copy(woven[:].rearrange("p (c i) t -> p c t i", i=4), hb[:, :, places].rearrange("p t (c i) -> p c t i", i=4))
             codes = held([P, HALF], U32, "codes%d" % h)
             plane = held([P, HALF], U8, "plane%d" % h)
             nc.vector.quantize_mx(codes[:].bitcast(FP8X4), plane[:], woven[:].rearrange("p c t -> p (c t)"))
 
-            def product(y, u):
-                nc.tensor.matmul_mx(y, lhsT=wb_codes[:, u * P : (u + 1) * P].bitcast(FP4X4), lhsT_scale=wb_plane[:, u * P : (u + 1) * P],
+            for u, copy, queue in ((0, nc.vector.tensor_copy, nc.sync), (1, nc.scalar.copy, nc.scalar)):
+                y = psum.tile([P, HALF], F32, name="y%d%d" % (h, u), tag="acc%d_0" % (2 * h + u))
+                nc.tensor.matmul_mx(y[:], lhsT=wb_codes[:, u * P : (u + 1) * P].bitcast(FP4X4), lhsT_scale=wb_plane[:, u * P : (u + 1) * P],
                                     rhs=codes[:].bitcast(FP8X4), rhs_scale=plane[:], start=True, stop=True)
-
-            if h == 0:
-                y = psum.tile([P, 2, HALF], F32, name="y0")
-                res = held([P, 2, HALF], F32, "res0")
-                for u in range(2):
-                    product(y[:, u, :], u)
-                nc.vector.tensor_copy(res[:], y[:])
-                nc.sync.dma_start(out_v[:, :, places], res[:])
-            else:
-                for u, copy, queue in ((0, nc.vector.tensor_copy, nc.sync), (1, nc.scalar.copy, nc.scalar)):
-                    y = psum.tile([P, HALF], F32, name="y1%d" % u)
-                    res = held([P, HALF], F32, "res1%d" % u)
-                    product(y[:], u)
-                    copy(res[:], y[:])
-                    queue.dma_start(out_v[:, u, places], res[:])
+                res = held([P, HALF], F32, "res%d%d" % (h, u))
+                copy(res[:], y[:])
+                queue.dma_start(out_v[:, u, places], res[:])

from contextlib import ExitStack

import concourse.mybir as mybir

K, J, R, T, Z, M, C, O, S, N = 512, 256, 512, 1024, 512, 1024, 512, 256, 128, 256
FLOPS = 2 * (K * R * J + Z * R * J + R * N * O)

F32 = mybir.dt.float32
BF16 = mybir.dt.bfloat16
I32 = mybir.dt.int32
U32 = mybir.dt.uint32
U16 = mybir.dt.uint16
U8 = mybir.dt.uint8
FP8X4 = mybir.dt.float8_e4m3fn_x4
FP4X4 = mybir.dt.float4_e2m1fn_x4
ALU = mybir.AluOpType
COPY = mybir.ActivationFunctionType.Copy
AX = mybir.AxisListType.X

P = 128
PACK = 4
HALF = O // 2
HALVES = ((slice(0, 128), slice(0, 8)), (slice(128, 256), slice(8, 16)))


def tile_picked_tokens_plain_bank_belowbest_one_plain_kernel(tc, xt_words, xt_scales, w_words, w_scales, xo_words, xo_scales, w2_words, w2_scales, sa, sb, wb_words, wb_scales, offs, offs2, offs3, offs4, offs5, offs6, out):
    nc = tc.nc
    with ExitStack() as ctx:
        keep = ctx.enter_context(tc.tile_pool(name="keep", bufs=1))
        psum = ctx.enter_context(tc.psum_pool(name="psum", bufs=1))

        def held(shape, dtype, name, tag=None):
            return keep.tile(shape, dtype, name=name, tag=tag or name, align_bytes=64)

        def load_list(src, name):
            lst = keep.tile([P, src.shape[1]], U16, name=name)
            nc.sync.dma_start(lst[:], src)
            return lst

        def zeroed_plane(width, name):
            plane = held([P, width], U8, name)
            nc.vector.memset(plane[:].bitcast(U32), 0)
            return plane

        def load_plane(plane, scales):
            for q in range(4):
                nc.sync.dma_start(plane[32 * q : 32 * q + 4, :].bitcast(I32), scales[0, 4 * q : 4 * q + 4, :].bitcast(I32))

        xt_plane = zeroed_plane(T, "xt_plane")
        ws_plane = zeroed_plane(2 * R, "ws_plane")
        xo_plane = zeroed_plane(M, "xo_plane")
        wb_plane = zeroed_plane(N, "wb_plane")
        ws_stage = held([4, 4, 2, R], U8, "ws_stage")

        xt_win = held([P, T], U16, "xt_win")
        xo_win = held([P, M], U32, "xo_win")
        w_raw = held([P, R], U32, "w_raw")
        w2_raw = held([P, R], U16, "w2_raw")
        wb_codes = held([P, N], U16, "wb_codes")
        sa_t = held([P, PACK], F32, "sa_t")
        sb_t = held([P, PACK], F32, "sb_t")

        def by_quadrant(scales):
            return scales[0].bitcast(I32).rearrange("(q i) c -> i q c", i=4)

        l1 = load_list(offs, "l1")
        nc.sync.dma_start(ws_stage[:, :, 0, :].bitcast(I32), by_quadrant(w_scales))
        nc.sync.dma_start(ws_stage[:, :, 1, :].bitcast(I32), by_quadrant(w2_scales))
        nc.sync.dma_start(xt_win[:].bitcast(I32), xt_words[0].bitcast(I32))
        l2 = load_list(offs2, "l2")
        nc.sync.dma_start(w_raw[:].bitcast(I32), w_words[0].rearrange("p n t -> p (n t)").bitcast(I32))
        load_plane(xt_plane, xt_scales)
        nc.sync.dma_start(xo_win[:].bitcast(I32), xo_words[0].rearrange("p n t -> p (n t)").bitcast(I32))
        nc.sync.dma_start(w2_raw[:].bitcast(I32), w2_words[0].bitcast(I32))
        load_plane(xo_plane, xo_scales)
        l3 = load_list(offs3, "l3")
        l4 = load_list(offs4, "l4")
        nc.sync.dma_start(sa_t[:], sa.rearrange("(p t) one -> p (t one)", t=PACK))
        l5 = load_list(offs5, "l5")
        l6 = load_list(offs6, "l6")
        nc.sync.dma_start(sb_t[:], sb.rearrange("(p t) one -> p (t one)", t=PACK))
        nc.sync.dma_start(wb_codes[:].bitcast(I32), wb_words[0].bitcast(I32))
        load_plane(wb_plane, wb_scales)

        xt_gs = held([P, J], U8, "xt_gs")
        xt_g = held([P, J], U16, "xt_g")
        xo_g = held([P, J], U32, "xo_g")
        xo_gs = held([P, J], U8, "xo_gs")
        for q in range(4):
            nc.vector.tensor_copy(ws_plane[32 * q : 32 * q + 4, :].bitcast(I32), ws_stage[:, q].rearrange("i w c -> i (w c)").bitcast(I32))
        nc.vector.tensor_copy(xt_g[:], xt_win[:].indirect(l1[:]))
        ws_first = held([P, 2, P], U8, "ws_first")
        ws_by_t = ws_plane[:].rearrange("p (w m t) -> p w t m", w=2, t=PACK)
        nc.vector.tensor_copy(ws_first[:], ws_by_t[:, :, 0, :])
        nc.vector.tensor_copy(xt_gs[:], xt_plane[:].indirect(l1[:]))
        for slots, entries in HALVES:
            nc.vector.tensor_copy(xo_g[:, slots], xo_win[:].indirect(l2[:, entries]))
            nc.vector.tensor_copy(xo_gs[:, slots], xo_plane[:].indirect(l2[:, entries]))

        dealt = []
        for raw, dtype, name in ((w_raw, U32, "w_d"), (w2_raw, U16, "w2_d")):
            first = held([P, P], dtype, name + "_first")
            rest = held([P, PACK - 1, P], dtype, name + "_rest")
            by_t = raw[:].rearrange("p (m t) -> p m t", t=PACK)
            nc.scalar.copy(first[:], by_t[:, :, 0])
            dealt.append((first, rest, by_t))

        def cols(i, t):
            if i >= 2:
                if t == 0:
                    return ws_first[:, i - 2, :]
                return ws_second[:, i - 2, :] if t == 1 else ws_rest[:, t - 2, i - 2, :]
            return dealt[i][0][:] if t == 0 else dealt[i][1][:, t - 1, :]

        a_tiles = []

        def hidden(t):
            a = held([P, J], F32, "a%d" % t)
            for i, slots in enumerate([h[0] for h in HALVES] if t == 0 else [slice(0, J)]):
                acc = psum.tile([P, slots.stop - slots.start], F32, name="acc%d_%d" % (t, i), tag="acc%d_%d" % (t, i))
                nc.tensor.matmul_mx(acc[:], lhsT=cols(0, t).bitcast(FP8X4), lhsT_scale=cols(2, t),
                                    rhs=xt_g[:, slots].bitcast(FP4X4), rhs_scale=xt_gs[:, slots], start=True, stop=False)
                nc.tensor.matmul_mx(acc[:], lhsT=cols(1, t).bitcast(FP4X4), lhsT_scale=cols(3, t),
                                    rhs=xo_g[:, slots].bitcast(FP8X4), rhs_scale=xo_gs[:, slots], start=False, stop=True)
                copy = nc.vector.tensor_copy
                copy(a[:, slots], acc[:])
            a_tiles.append(a)

        hidden(0)
        for first, rest, by_t in dealt:
            nc.scalar.copy(rest[:].rearrange("p t m -> p m t"), by_t[:, :, 1:PACK])
        ws_second = held([P, 2, P], U8, "ws_second", "ws_first")
        ws_rest = held([P, 2, 2, P], U8, "ws_rest", "w2_d_first")
        def zeroed_board(name, tag):
            board = held([P, C], F32, name, tag)
            nc.vector.memset(board[:].bitcast(I32), 0)
            return board

        pw_boards = [zeroed_board("pw0", "pw0")]
        pv_boards = [zeroed_board("pv0", "pv0")]
        for t in range(1, PACK):
            nc.vector.tensor_copy(ws_second[:] if t == 1 else ws_rest[:, t - 2], ws_by_t[:, :, t, :])
            hidden(t)
            if t == 1:
                pw_boards.append(zeroed_board("pw1", "pw1"))
        pv_boards.append(zeroed_board("pv1", "w2_d_first"))

        pw_tiles, h1_tiles, pb_tiles, pg_tiles = {}, {}, {}, {}

        def put_board(t, slots=slice(0, J), entries=slice(0, J // 16)):
            pw = pw_boards[t % 2]
            nc.scalar.activation(pw[:].indirect(l3[:, entries]), a_tiles[t][:, slots], COPY)
            pw_tiles[t] = pw

        def fetch_marks(t):
            h1 = held([P, S], F32, "h1_%d" % t)
            nc.scalar.activation(h1[:], a_tiles[t][:].indirect(l4[:]), COPY, scale=sa_t[:, t : t + 1])
            top = held([P, 1], F32, "top%d" % t, "ws_first" if t == 0 else "w_d_rest")
            pb = held([P, 1], F32, "pb%d" % t)
            nc.vector.tensor_reduce(top[:], h1[:], AX, ALU.max)
            nc.vector.tensor_scalar(pb[:], top[:], 0.0, None, ALU.max)
            h1_tiles[t], pb_tiles[t] = h1, pb

        pv_tiles = {}

        def put_marks(t):
            pv = pv_boards[t % 2]
            nc.scalar.activation(pv[:].indirect(l5[:]), h1_tiles[t][:], COPY)
            pv_tiles[t] = pv

        def join(t):
            pg = held([P, C], F32, "pg%d" % t)
            nc.vector.scalar_tensor_tensor(pg[:], pv_tiles[t][:], pb_tiles[t][:], pw_tiles[t][:], ALU.subtract, ALU.max)
            pg_tiles[t] = pg

        put_board(0, *HALVES[0])
        fetch_marks(0)
        put_board(0, *HALVES[1])
        put_marks(0)
        join(0)
        fetch_marks(1)
        put_board(1)
        put_marks(1)
        join(1)
        fetch_marks(2)
        put_board(2)
        fetch_marks(3)
        put_marks(2)
        join(2)
        put_marks(3)
        put_board(3)
        join(3)

        out_v = out.rearrange("(u p) o -> p u o", p=P)
        hb = held([P, PACK, O], BF16, "hb", "h1_3")
        for t in range(PACK - 1):
            nc.scalar.activation(hb[:, t, :], pg_tiles[t][:].indirect(l6[:]), COPY, scale=sb_t[:, t : t + 1])
        for h, (places, entries) in enumerate(HALVES):
            nc.scalar.activation(hb[:, PACK - 1, places], pg_tiles[PACK - 1][:].indirect(l6[:, entries]), COPY, scale=sb_t[:, PACK - 1 : PACK])
            woven = held([P, HALF, PACK], BF16, "woven%d" % h)
            nc.vector.tensor_copy(woven[:].rearrange("p (c i) t -> p c t i", i=4), hb[:, :, places].rearrange("p t (c i) -> p c t i", i=4))
            codes = held([P, HALF], U32, "codes%d" % h)
            plane = held([P, HALF], U8, "plane%d" % h)
            nc.vector.quantize_mx(codes[:].bitcast(FP8X4), plane[:], woven[:].rearrange("p c t -> p (c t)"))

            for u, copy, queue in ((0, nc.vector.tensor_copy, nc.sync), (1, nc.scalar.copy, nc.scalar)):
                y = psum.tile([P, HALF], F32, name="y%d%d" % (h, u), tag="acc%d_0" % (2 * h + u))
                nc.tensor.matmul_mx(y[:], lhsT=wb_codes[:, u * P : (u + 1) * P].bitcast(FP4X4), lhsT_scale=wb_plane[:, u * P : (u + 1) * P],
                                    rhs=codes[:].bitcast(FP8X4), rhs_scale=plane[:], start=True, stop=True)
                res = held([P, HALF], F32, "res%d%d" % (h, u))
                copy(res[:], y[:])
                queue.dma_start(out_v[:, u, places], res[:])
